import numpy as np
import ml_dtypes


def mxq(x, axis, fmt="e4m3"):
    dtype, down = {"e4m3": (ml_dtypes.float8_e4m3fn, 7), "e5m2": (ml_dtypes.float8_e5m2, 14)}[fmt]
    v = np.moveaxis(np.asarray(x, np.float32).astype(ml_dtypes.bfloat16).astype(np.float64), axis, -1)
    blocks = v.reshape(v.shape[:-1] + (-1, 32))
    amax = np.abs(blocks).max(-1, keepdims=True)
    byte = np.maximum(np.where(amax > 0, np.frexp(amax)[1] - 1 + 127, 0) - down, 1)
    scale = np.exp2(byte - 127.0)
    codes = (blocks / scale).astype(np.float32).astype(dtype).astype(np.float64)
    return np.moveaxis((codes * scale).reshape(v.shape), -1, axis)


WIDE = False


def mx_kscale(k):
    if not WIDE:
        return np.ones(k)
    levels = np.array([10, -10, 5, -5, 0])
    if k % 512:
        return np.exp2(np.random.permutation(np.resize(levels, k // 32))).repeat(32)
    a = np.empty((k // 512, 16))
    for p in range(k // 512):
        a[p, :8] = np.random.permutation(np.resize(levels, 8))
        for g in range(8):
            far = levels[np.abs(levels - a[p, g]) >= 10]
            a[p, g + 8] = far[np.random.randint(len(far))]
    return np.exp2(a.ravel()).repeat(32)


def f64(x):
    return np.asarray(x).astype(np.float64)


def striped(idx):
    return np.tile(np.asarray(idx).reshape(-1, 16).T, (8, 1)).astype(np.uint16)


def unstriped(offs):
    return offs[:16].T.reshape(-1).astype(np.int64)


E2M1 = np.array([0.0, 0.5, 1.0, 1.5, 2.0, 3.0, 4.0, 6.0, -0.0, -0.5, -1.0, -1.5, -2.0, -3.0, -4.0, -6.0])


def pack_weight(w, fmt):
    k, n = w.shape
    w = f64(np.asarray(w, np.float32).astype(ml_dtypes.bfloat16)).reshape(k // 32, 32, n)
    amax = np.abs(w).max(1)
    if fmt == "e4m3":
        byte = np.frexp(amax)[1] - 1 + 127 - 7
    else:
        mant, ex = np.frexp(amax / 6.0)
        byte = np.where(mant > 0.5, ex, ex - 1) + 127
    byte = np.clip(np.where(amax > 0, byte, 1), 1, 254)
    scaled = (w * np.exp2(127.0 - byte)[:, None, :]).reshape(k, n).astype(np.float32)
    by_word = np.ascontiguousarray(scaled.reshape(k // 512, 128, 4, n).transpose(0, 1, 3, 2))
    if fmt == "e4m3":
        words = by_word.astype(ml_dtypes.float8_e4m3fn).view(np.uint8)
    else:
        c = by_word.astype(ml_dtypes.float4_e2m1fn).view(np.uint8) & 0xF
        words = (c[..., 0::2] | (c[..., 1::2] << 4)).reshape(k // 512, 128, 2 * n)
    return np.ascontiguousarray(words), np.ascontiguousarray(byte.astype(np.uint8).reshape(k // 512, 16, n))


def unpack_weight(words, scales, fmt):
    g, _, n = scales.shape
    words = np.ascontiguousarray(words).reshape(g, 128, n, -1)
    if fmt == "e4m3":
        vals = words.view(ml_dtypes.float8_e4m3fn).astype(np.float64)
    else:
        nib = np.empty((g, 128, n, 4), np.uint8)
        nib[..., 0::2] = words & 0xF
        nib[..., 1::2] = words >> 4
        vals = E2M1[nib]
    vals = vals * np.repeat(np.exp2(scales.astype(np.float64) - 127.0), 8, axis=1)[..., None]
    return vals.transpose(0, 1, 3, 2).reshape(g * 512, n)


D, E, T, I, Q = 512, 512, 1024, 256, 512


def setup_inputs():
    n = np.random.standard_normal
    idx = np.random.permutation(T)[:I]
    idx2 = np.random.permutation(T)[:I]
    fd = mx_kscale(D)
    fq = mx_kscale(Q)
    keysp = pack_weight(n((D, T)) / fd[:, None], "e2m1")
    return {
        "query": (n((D, Q)) * 0.5 / np.sqrt(D) * fd[:, None]).astype(np.float32),
        "qs": (np.random.uniform(8.0, 32.0, (Q, 1)) * fq[:, None]).astype(np.float32),
        "grows": (n((Q, E)) / fq[:, None]).astype(np.float32),
        "keys_words": keysp[0],
        "keys_scales": keysp[1],
        "cross": (n((E, T))).astype(np.float32),
        "share": (np.random.uniform(0.4, 1.2, (E, 1))).astype(np.float32),
        "sg": (np.random.uniform(0.5, 2.0, (1, I))).astype(np.float32),
        "old": (n((E, T)) * 1.0).astype(np.float32),
        "fade": (np.random.uniform(0.5, 1.0, (1, T))).astype(np.float32),
        "offs": striped(idx),
        "offs2": striped(idx2),
    }


def reference(query, qs, grows, keys_words, keys_scales, cross, share, sg, old, fade, offs, offs2):
    idx = unstriped(offs)
    idx2 = unstriped(offs2)
    keysu = unpack_weight(keys_words, keys_scales, "e2m1")
    queryq = mxq(f64(query), 0, "e4m3")
    keysidxg = keysu[:, idx]
    a = queryq.T @ keysidxg
    p = np.exp(a - np.max(a, axis=1, keepdims=True))
    w = p * f64(qs) / np.sum(p, axis=1, keepdims=True)
    growsq = mxq(f64(grows), 0, "e4m3")
    wq = mxq(w, 0, "e4m3")
    c0 = growsq.T @ wq
    dx1 = c0 * f64(cross)[:, idx2] + c0 * f64(share)
    gs = dx1 * f64(sg)
    gf = np.zeros((E, T))
    gf[:, idx] = gs
    y = f64(old) * f64(fade) + gf
    return y

@@ -1,0 +1,212 @@
+from contextlib import ExitStack
+
+import concourse.mybir as mybir
+from concourse.masks import make_identity
+
+D, E, T, I, Q = 512, 512, 1024, 256, 512
+FLOPS = 2 * D * Q * I + 2 * Q * E * I
+
+F32 = mybir.dt.float32
+BF16 = mybir.dt.bfloat16
+I32 = mybir.dt.int32
+U32 = mybir.dt.uint32
+U16 = mybir.dt.uint16
+U8 = mybir.dt.uint8
+FP8X4 = mybir.dt.float8_e4m3fn_x4
+FP4X4 = mybir.dt.float4_e2m1fn_x4
+ACT = mybir.ActivationFunctionType
+ALU = mybir.AluOpType
+AXIS = mybir.AxisListType
+
+P = 128
+PACK = 4
+HALF = 512
+
+
+def tile_attend_bvcrossed_s_kernel(tc, query, qs, grows, keys_words, keys_scales, cross, share, sg, old, fade, offs, offs2, out):
+    nc = tc.nc
+    with ExitStack() as ctx:
+        lists = ctx.enter_context(tc.tile_pool(name="lists", bufs=1))
+        keep = ctx.enter_context(tc.tile_pool(name="keep", bufs=1))
+        psum = ctx.enter_context(tc.psum_pool(name="psum", bufs=1))
+        psum2 = ctx.enter_context(tc.psum_pool(name="psum2", bufs=2))
+
+        key_scales = keep.tile([P, T], U8, name="key_scales", align_bytes=64)
+        nc.gpsimd.memset(key_scales[:].bitcast(I32), 0)
+        warm = keep.tile([P, 1], F32, name="warm")
+        nc.gpsimd.memset(warm[:], 0.0)
+        rows = keep.tile([P, P], F32, name="rows")
+        nc.gpsimd.memset(rows[:], 0.0)
+        key_words = keep.tile([P, T], U16, name="key_words", align_bytes=64)
+        nc.sync.dma_start(out=key_words[:].bitcast(I32), in_=keys_words[0].bitcast(I32))
+        offs_t = lists.tile([P, I // 16], U16, name="offs_t")
+        nc.sync.dma_start(offs_t[:], offs)
+        for quad in range(4):
+            nc.sync.dma_start(out=key_scales[32 * quad : 32 * quad + 4, :].bitcast(I32), in_=keys_scales[0, 4 * quad : 4 * quad + 4, :].bitcast(I32))
+        q_view = query.rearrange("(p j) q -> p j q", j=PACK)
+        q_raw = []
+        for h in range(2):
+            t = keep.tile([P, PACK, Q // 2], F32, name=f"q_raw{h}")
+            nc.sync.dma_start(out=t[:], in_=q_view[:, :, h * (Q // 2) : (h + 1) * (Q // 2)])
+            q_raw.append(t)
+        nc.sync.dma_start(out=rows[0:8, :], in_=fade.rearrange("o (b t) -> (o b) t", t=P))
+        nc.sync.dma_start(out=rows[8:12, :], in_=share.rearrange("(j p) o -> j (p o)", p=P))
+        nc.sync.dma_start(out=rows[12:14, :], in_=sg.rearrange("o (b t) -> (o b) t", t=P))
+        qs_t = keep.tile([P, PACK], F32, name="qs_t")
+        nc.sync.dma_start(out=qs_t[:], in_=qs.rearrange("(p r) o -> p (r o)", r=PACK))
+        offs2_t = lists.tile([P, I // 16], U16, name="offs2_t")
+        nc.sync.dma_start(offs2_t[:], offs2)
+        cross_t = [keep.tile([P, T], F32, name=f"cross{j}") for j in range(4)]
+        old_t = [keep.tile([P, T], F32, name=f"old{j}") for j in range(4)]
+        nc.sync.dma_start(out=cross_t[0][:], in_=cross[0:P, :])
+        g_raw = keep.tile([P, PACK, E], F32, name="g_raw")
+        nc.sync.dma_start(out=g_raw[:], in_=grows.rearrange("(p r) e -> p r e", r=PACK))
+        for j in range(4):
+            if j < 3:
+                nc.sync.dma_start(out=cross_t[j + 1][:], in_=cross[P * (j + 1) : P * (j + 2), :])
+            nc.sync.dma_start(out=old_t[j][:], in_=old[P * j : P * (j + 1), :])
+
+        nc.scalar.activation(warm[:], warm[:], ACT.Exp)
+        ident = keep.tile([P, P], F32, name="ident")
+        make_identity(nc, ident[:])
+        gf = []
+        for j in range(2):
+            g = keep.tile([P, T], F32, name=f"gf{j}")
+            nc.gpsimd.memset(g[:], 0.0)
+            gf.append(g)
+
+        kg = keep.tile([P, I], U16, name="kg", align_bytes=64)
+        nc.vector.tensor_copy(kg[:], key_words[:].indirect(offs_t[:]))
+        ksg = keep.tile([P, I], U8, name="ksg", align_bytes=64)
+        nc.vector.tensor_copy(ksg[:], key_scales[:].indirect(offs_t[:]))
+
+        q_bf = keep.tile([P, PACK, P, PACK], BF16, name="q_bf", align_bytes=64)
+        for h, s0, s1, copy in ((0, 0, 64, nc.scalar.copy), (1, 0, 44, nc.vector.tensor_copy), (1, 44, 64, nc.scalar.copy)):
+            dst = q_bf[:, :, 64 * h + s0 : 64 * h + s1, :].rearrange("p r s j -> p s j r")
+            src = q_raw[h][:, :, PACK * s0 : PACK * s1].rearrange("p j (s r) -> p s j r", r=PACK)
+            copy(dst, src)
+        small = psum2.tile([P, HALF], F32, name="small", tag="fwd")
+        nc.tensor.transpose(small[:, 0:P], rows[:], ident[:])
+        cols_t = keep.tile([P, 16], F32, name="cols_t")
+        nc.scalar.copy(cols_t[:], small[:, 0:16])
+        spread = psum2.tile([P, HALF], F32, name="spread", tag="fwd")
+        for c in range(2):
+            nc.tensor.transpose(spread[:, P * c : P * (c + 1)], cols_t[:, 12 + c : 13 + c].to_broadcast([P, P]), ident[:])
+        sg_t = keep.tile([P, I], F32, name="sg_t")
+        nc.scalar.copy(sg_t[:], spread[:, 0:I])
+
+        q_codes = keep.tile([P, Q], U32, name="q_codes", align_bytes=64)
+        q_scales = keep.tile([P, Q], U8, name="q_scales", align_bytes=64)
+        negmax = keep.tile([P, PACK], F32, name="negmax")
+        sums = keep.tile([P, PACK], F32, name="sums")
+        p_t = keep.tile([P, PACK, I], F32, name="p_t")
+        scores = []
+        for r in range(PACK):
+            cols = slice(P * r, P * (r + 1))
+            nc.vector.quantize_mx(out=q_codes[:, cols].bitcast(FP8X4), scales=q_scales[:, cols], in_=q_bf[:, r].rearrange("p s j -> p (s j)"))
+            a = psum.tile([P, I], F32, name=f"bank{r}", tag=f"bank{r}")
+            nc.tensor.matmul_mx(out=a[:], lhsT=q_codes[:, cols].bitcast(FP8X4), lhsT_scale=q_scales[:, cols], rhs=kg[:].bitcast(FP4X4), rhs_scale=ksg[:], start=True, stop=True)
+            scores.append(a)
+        for r in range(PACK):
+            nc.vector.tensor_reduce(negmax[:, r : r + 1], scores[r][:], AXIS.X, ALU.max, negate=True)
+            nc.scalar.activation(p_t[:, r, :], scores[r][:], ACT.Exp, bias=negmax[:, r : r + 1], scale=1.0, accum_out=sums[:, r : r + 1])
+
+        g_bf = keep.tile([P, E, PACK], BF16, name="g_bf", align_bytes=64)
+        g_codes = keep.tile([P, E], U32, name="g_codes", align_bytes=64)
+        g_scales = keep.tile([P, E], U8, name="g_scales", align_bytes=64)
+
+        def grows_block(j):
+            cols = slice(P * j, P * (j + 1))
+            nc.scalar.copy(g_bf[:, cols, :].rearrange("p (c i) r -> p c r i", i=4), g_raw[:, :, cols].rearrange("p r (c i) -> p c r i", i=4))
+            nc.vector.quantize_mx(out=g_codes[:, cols].bitcast(FP8X4), scales=g_scales[:, cols], in_=g_bf[:, cols, :].rearrange("p e r -> p (e r)"))
+
+        cg = {}
+
+        def gather(j):
+            cg[j] = keep.tile([P, I], F32, name=f"cg{j}")
+            nc.vector.tensor_copy(cg[j][:], cross_t[j][:].indirect(offs2_t[:]))
+
+        rinv = keep.tile([P, PACK], F32, name="rinv")
+        w_rows = keep.tile([P, PACK, I], BF16, name="w_rows")
+        for r0 in (0, 2):
+            nc.vector.reciprocal(rinv[:, r0 : r0 + 2], sums[:, r0 : r0 + 2])
+            if r0 == 0:
+                gather(0)
+            for r in (r0, r0 + 1):
+                nc.vector.tensor_scalar(w_rows[:, r, :], p_t[:, r, :], rinv[:, r : r + 1], qs_t[:, r : r + 1], ALU.mult, ALU.mult)
+        grows_block(0)
+        w_bf = keep.tile([P, I, PACK], BF16, name="w_bf", align_bytes=64)
+        nc.vector.tensor_copy(w_bf[:].rearrange("p (c i) r -> p c r i", i=4), w_rows[:].rearrange("p r (c i) -> p c r i", i=4))
+        w_codes = keep.tile([P, I], U32, name="w_codes", align_bytes=64)
+        w_scales = keep.tile([P, I], U8, name="w_scales", align_bytes=64)
+        nc.vector.quantize_mx(out=w_codes[:].bitcast(FP8X4), scales=w_scales[:], in_=w_bf[:].rearrange("p i r -> p (i r)"))
+
+        c0, dx, back, res, faded_t = {}, {}, {}, {}, {}
+        window = (gf[0], gf[1], gf[0], gf[0])
+
+        def product(j):
+            cols = slice(P * j, P * (j + 1))
+            c0[j] = psum.tile([P, I], F32, name=f"c0_{j}", tag=f"bank{j % 2}")
+            nc.tensor.matmul_mx(out=c0[j][:], lhsT=g_codes[:, cols].bitcast(FP8X4), lhsT_scale=g_scales[:, cols], rhs=w_codes[:].bitcast(FP8X4), rhs_scale=w_scales[:], start=True, stop=True)
+
+        def chain(j):
+            dx[j] = keep.tile([P, I], F32, name=f"dx{j}")
+            nc.vector.scalar_tensor_tensor(dx[j][:], cg[j][:], cols_t[:, 8 + j : 9 + j], c0[j][:], ALU.add, ALU.mult)
+
+        def scatter(j):
+            nc.vector.tensor_tensor(window[j][:].indirect(offs_t[:]), dx[j][:], sg_t[:], ALU.mult)
+
+        def faded(j):
+            for h in range(2):
+                fwd = psum2.tile([P, HALF], F32, name="fwd", tag="fwd")
+                for b in range(4):
+                    nc.tensor.transpose(fwd[:, P * b : P * (b + 1)], old_t[j][:, HALF * h + P * b : HALF * h + P * (b + 1)], ident[:])
+                faded_t[j, h] = keep.tile([P, HALF], F32, name=f"faded_t{j}{h}")
+                for b in range(4):
+                    nc.scalar.activation(faded_t[j, h][:, P * b : P * (b + 1)], fwd[:, P * b : P * (b + 1)], ACT.Copy, scale=cols_t[:, 4 * h + b : 4 * h + b + 1])
+
+        def turn_back(j):
+            for h in range(2):
+                back[j, h] = psum.tile([P, HALF], F32, name=f"back{j}{h}", tag=f"bank{4 + h - 2 * (j % 2)}")
+                for b in range(4):
+                    nc.tensor.transpose(back[j, h][:, P * b : P * (b + 1)], faded_t[j, h][:, P * b : P * (b + 1)], ident[:])
+
+        def finish(j):
+            cols = slice(P * j, P * (j + 1))
+            res[j] = keep.tile([P, T], F32, name=f"res{j}")
+            edges = (0, 512, 768, 1024) if j == 3 else (0, 512, 1024)
+            for a, b in zip(edges, edges[1:]):
+                h = a // HALF
+                nc.vector.tensor_tensor(res[j][:, a:b], back[j, h][:, a - HALF * h : b - HALF * h], window[j][:, a:b], ALU.add)
+                nc.sync.dma_start(out=out[cols, a:b], in_=res[j][:, a:b])
+
+        product(0)
+        gather(1)
+        grows_block(1)
+        product(1)
+        chain(0)
+        chain(1)
+        grows_block(2)
+        grows_block(3)
+        product(2)
+        product(3)
+        faded(0)
+        turn_back(0)
+        faded(1)
+        turn_back(1)
+        scatter(0)
+        scatter(1)
+        finish(0)
+        gather(2)
+        faded(2)
+        turn_back(2)
+        chain(2)
+        gather(3)
+        scatter(2)
+        finish(1)
+        faded(3)
+        turn_back(3)
+        chain(3)
+        finish(2)
+        scatter(3)
+        finish(3)

@@ -52,25 +52,26 @@ def tile_attend_bvcrossed_s_kernel(tc, query, qs, grows, keys_words, keys_scales
         nc.sync.dma_start(out=rows[0:8, :], in_=fade.rearrange("o (b t) -> (o b) t", t=P))
         nc.sync.dma_start(out=rows[8:12, :], in_=share.rearrange("(j p) o -> j (p o)", p=P))
         nc.sync.dma_start(out=rows[12:14, :], in_=sg.rearrange("o (b t) -> (o b) t", t=P))
-        qs_t = keep.tile([P, PACK], F32, name="qs_t")
-        nc.sync.dma_start(out=qs_t[:], in_=qs.rearrange("(p r) o -> p (r o)", r=PACK))
+        nc.sync.dma_start(out=rows[16:20, :].rearrange("r (b c) -> r b c", c=8), in_=qs.rearrange("(b r c) o -> r b (c o)", r=PACK, c=8))
         offs2_t = lists.tile([P, I // 16], U16, name="offs2_t")
         nc.sync.dma_start(offs2_t[:], offs2)
         cross_t = [keep.tile([P, T], F32, name=f"cross{j}") for j in range(4)]
         old_t = [keep.tile([P, T], F32, name=f"old{j}") for j in range(4)]
         nc.sync.dma_start(out=cross_t[0][:], in_=cross[0:P, :])
         g_raw = keep.tile([P, PACK, E], F32, name="g_raw")
-        nc.sync.dma_start(out=g_raw[:], in_=grows.rearrange("(p r) e -> p r e", r=PACK))
+        g_view = grows.rearrange("(b r c) e -> r b c e", r=PACK, c=8)
+        for r in range(PACK):
+            nc.sync.dma_start(out=g_raw[:, r, :], in_=g_view[r])
+        for j in range(1, 4):
+            nc.sync.dma_start(out=cross_t[j][:], in_=cross[P * j : P * (j + 1), :])
         for j in range(4):
-            if j < 3:
-                nc.sync.dma_start(out=cross_t[j + 1][:], in_=cross[P * (j + 1) : P * (j + 2), :])
             nc.sync.dma_start(out=old_t[j][:], in_=old[P * j : P * (j + 1), :])
 
         nc.scalar.activation(warm[:], warm[:], ACT.Exp)
         ident = keep.tile([P, P], F32, name="ident")
         make_identity(nc, ident[:])
         gf = []
-        for j in range(2):
+        for j in range(3):
             g = keep.tile([P, T], F32, name=f"gf{j}")
             nc.gpsimd.memset(g[:], 0.0)
             gf.append(g)
@@ -81,19 +82,15 @@ def tile_attend_bvcrossed_s_kernel(tc, query, qs, grows, keys_words, keys_scales
         nc.vector.tensor_copy(ksg[:], key_scales[:].indirect(offs_t[:]))
 
         q_bf = keep.tile([P, PACK, P, PACK], BF16, name="q_bf", align_bytes=64)
-        for h, s0, s1, copy in ((0, 0, 64, nc.scalar.copy), (1, 0, 44, nc.vector.tensor_copy), (1, 44, 64, nc.scalar.copy)):
-            dst = q_bf[:, :, 64 * h + s0 : 64 * h + s1, :].rearrange("p r s j -> p s j r")
-            src = q_raw[h][:, :, PACK * s0 : PACK * s1].rearrange("p j (s r) -> p s j r", r=PACK)
+        def deal(copy, h, r):
+            dst = q_bf[:, r, 64 * h : 64 * (h + 1), :].rearrange("p (b c i) j -> p b c j i", c=2, i=4)
+            src = q_raw[h][:].rearrange("p j (b r c i) -> p r b c j i", r=PACK, c=2, i=4)[:, r]
             copy(dst, src)
-        small = psum2.tile([P, HALF], F32, name="small", tag="fwd")
-        nc.tensor.transpose(small[:, 0:P], rows[:], ident[:])
-        cols_t = keep.tile([P, 16], F32, name="cols_t")
-        nc.scalar.copy(cols_t[:], small[:, 0:16])
-        spread = psum2.tile([P, HALF], F32, name="spread", tag="fwd")
-        for c in range(2):
-            nc.tensor.transpose(spread[:, P * c : P * (c + 1)], cols_t[:, 12 + c : 13 + c].to_broadcast([P, P]), ident[:])
-        sg_t = keep.tile([P, I], F32, name="sg_t")
-        nc.scalar.copy(sg_t[:], spread[:, 0:I])
+
+        for r in range(PACK):
+            deal(nc.scalar.copy, 0, r)
+        deal(nc.scalar.copy, 1, 3)
+        deal(nc.vector.tensor_copy, 1, 0)
 
         q_codes = keep.tile([P, Q], U32, name="q_codes", align_bytes=64)
         q_scales = keep.tile([P, Q], U8, name="q_scales", align_bytes=64)
@@ -103,13 +100,22 @@ def tile_attend_bvcrossed_s_kernel(tc, query, qs, grows, keys_words, keys_scales
         scores = []
         for r in range(PACK):
             cols = slice(P * r, P * (r + 1))
+            if r < 2:
+                deal(nc.vector.tensor_copy, 1, r + 1)
             nc.vector.quantize_mx(out=q_codes[:, cols].bitcast(FP8X4), scales=q_scales[:, cols], in_=q_bf[:, r].rearrange("p s j -> p (s j)"))
-            a = psum.tile([P, I], F32, name=f"bank{r}", tag=f"bank{r}")
-            nc.tensor.matmul_mx(out=a[:], lhsT=q_codes[:, cols].bitcast(FP8X4), lhsT_scale=q_scales[:, cols], rhs=kg[:].bitcast(FP4X4), rhs_scale=ksg[:], start=True, stop=True)
+            a = psum.tile([P, HALF], F32, name=f"bank{r}", tag=f"bank{r}")
+            nc.tensor.matmul_mx(out=a[:, 0:I], lhsT=q_codes[:, cols].bitcast(FP8X4), lhsT_scale=q_scales[:, cols], rhs=kg[:].bitcast(FP4X4), rhs_scale=ksg[:], start=True, stop=True)
             scores.append(a)
+        nc.tensor.transpose(scores[3][:, I : I + P], rows[:], ident[:])
+        cols_t = keep.tile([P, 20], F32, name="cols_t")
+        nc.scalar.copy(cols_t[:], scores[3][:, I : I + 20])
+        spread = psum.tile([P, 2, I], F32, name="spread", tag="bank5")
+        for c in range(2):
+            nc.tensor.transpose(spread[:, 0, P * c : P * (c + 1)], cols_t[:, 12 + c : 13 + c].to_broadcast([P, P]), ident[:])
+
         for r in range(PACK):
-            nc.vector.tensor_reduce(negmax[:, r : r + 1], scores[r][:], AXIS.X, ALU.max, negate=True)
-            nc.scalar.activation(p_t[:, r, :], scores[r][:], ACT.Exp, bias=negmax[:, r : r + 1], scale=1.0, accum_out=sums[:, r : r + 1])
+            nc.vector.tensor_reduce(negmax[:, r : r + 1], scores[r][:, 0:I], AXIS.X, ALU.max, negate=True)
+            nc.scalar.activation(p_t[:, r, :], scores[r][:, 0:I], ACT.Exp, bias=negmax[:, r : r + 1], scale=1.0, accum_out=sums[:, r : r + 1])
 
         g_bf = keep.tile([P, E, PACK], BF16, name="g_bf", align_bytes=64)
         g_codes = keep.tile([P, E], U32, name="g_codes", align_bytes=64)
@@ -126,6 +132,12 @@ def tile_attend_bvcrossed_s_kernel(tc, query, qs, grows, keys_words, keys_scales
             cg[j] = keep.tile([P, I], F32, name=f"cg{j}")
             nc.vector.tensor_copy(cg[j][:], cross_t[j][:].indirect(offs2_t[:]))
 
+        fac = {}
+
+        def factor(j):
+            fac[j] = keep.tile([P, I], F32, name=f"fac{j}")
+            nc.vector.scalar_tensor_tensor(fac[j][:], cg[j][:], cols_t[:, 8 + j : 9 + j], spread[:, 0, :], ALU.add, ALU.mult)
+
         rinv = keep.tile([P, PACK], F32, name="rinv")
         w_rows = keep.tile([P, PACK, I], BF16, name="w_rows")
         for r0 in (0, 2):
@@ -133,28 +145,35 @@ def tile_attend_bvcrossed_s_kernel(tc, query, qs, grows, keys_words, keys_scales
             if r0 == 0:
                 gather(0)
             for r in (r0, r0 + 1):
-                nc.vector.tensor_scalar(w_rows[:, r, :], p_t[:, r, :], rinv[:, r : r + 1], qs_t[:, r : r + 1], ALU.mult, ALU.mult)
-        grows_block(0)
+                nc.vector.tensor_scalar(w_rows[:, r, :], p_t[:, r, :], rinv[:, r : r + 1], cols_t[:, 16 + r : 17 + r], ALU.mult, ALU.mult)
+        factor(0)
         w_bf = keep.tile([P, I, PACK], BF16, name="w_bf", align_bytes=64)
         nc.vector.tensor_copy(w_bf[:].rearrange("p (c i) r -> p c r i", i=4), w_rows[:].rearrange("p r (c i) -> p c r i", i=4))
+        grows_block(0)
         w_codes = keep.tile([P, I], U32, name="w_codes", align_bytes=64)
         w_scales = keep.tile([P, I], U8, name="w_scales", align_bytes=64)
         nc.vector.quantize_mx(out=w_codes[:].bitcast(FP8X4), scales=w_scales[:], in_=w_bf[:].rearrange("p i r -> p (i r)"))
 
-        c0, dx, back, res, faded_t = {}, {}, {}, {}, {}
-        window = (gf[0], gf[1], gf[0], gf[0])
+        c0, dx, back, res, faded_t, kept = {}, {}, {}, {}, {}, {}
+        window = (gf[0], gf[1], gf[2], gf[0])
 
         def product(j):
             cols = slice(P * j, P * (j + 1))
-            c0[j] = psum.tile([P, I], F32, name=f"c0_{j}", tag=f"bank{j % 2}")
-            nc.tensor.matmul_mx(out=c0[j][:], lhsT=g_codes[:, cols].bitcast(FP8X4), lhsT_scale=g_scales[:, cols], rhs=w_codes[:].bitcast(FP8X4), rhs_scale=w_scales[:], start=True, stop=True)
+            if j == 1:
+                pair = psum.tile([P, 2, I], F32, name="c0_pair", tag="bank1")
+                c0[1], c0[2] = pair[:, 0, :], pair[:, 1, :]
+            elif j == 0:
+                c0[j] = psum.tile([P, I], F32, name="c0_first", tag="bank0")[:]
+            elif j == 3:
+                c0[j] = spread[:, 1, :]
+            nc.tensor.matmul_mx(out=c0[j], lhsT=g_codes[:, cols].bitcast(FP8X4), lhsT_scale=g_scales[:, cols], rhs=w_codes[:].bitcast(FP8X4), rhs_scale=w_scales[:], start=True, stop=True)
 
         def chain(j):
             dx[j] = keep.tile([P, I], F32, name=f"dx{j}")
-            nc.vector.scalar_tensor_tensor(dx[j][:], cg[j][:], cols_t[:, 8 + j : 9 + j], c0[j][:], ALU.add, ALU.mult)
+            nc.vector.tensor_tensor(dx[j][:], c0[j], fac[j][:], ALU.mult)
 
         def scatter(j):
-            nc.vector.tensor_tensor(window[j][:].indirect(offs_t[:]), dx[j][:], sg_t[:], ALU.mult)
+            nc.vector.tensor_copy(window[j][:].indirect(offs_t[:]), dx[j][:])
 
         def faded(j):
             for h in range(2):
@@ -165,11 +184,25 @@ def tile_attend_bvcrossed_s_kernel(tc, query, qs, grows, keys_words, keys_scales
                 for b in range(4):
                     nc.scalar.activation(faded_t[j, h][:, P * b : P * (b + 1)], fwd[:, P * b : P * (b + 1)], ACT.Copy, scale=cols_t[:, 4 * h + b : 4 * h + b + 1])
 
+        def faded_on_gpsimd(j):
+            fade_row = keep.tile([P, T], F32, name="fade_row")
+            for h in range(2):
+                fwd = psum2.tile([P, HALF], F32, name="fwd", tag="fwd")
+                for b in range(4):
+                    nc.tensor.transpose(fwd[:, P * b : P * (b + 1)], cols_t[:, 4 * h + b : 4 * h + b + 1].to_broadcast([P, P]), ident[:])
+                half = slice(HALF * h, HALF * (h + 1))
+                nc.scalar.copy(fade_row[:, half], fwd[:])
+                kept[j, h] = keep.tile([P, HALF], F32, name=f"kept{j}{h}")
+                nc.gpsimd.tensor_tensor(kept[j, h][:], old_t[j][:, half], fade_row[:, half], ALU.mult)
+
         def turn_back(j):
             for h in range(2):
-                back[j, h] = psum.tile([P, HALF], F32, name=f"back{j}{h}", tag=f"bank{4 + h - 2 * (j % 2)}")
+                back[j, h] = psum.tile([P, HALF], F32, name=f"back{j}{h}", tag=f"bank{2 + (2 * j + h) % 3}")
                 for b in range(4):
                     nc.tensor.transpose(back[j, h][:, P * b : P * (b + 1)], faded_t[j, h][:, P * b : P * (b + 1)], ident[:])
+                if j < 3:
+                    kept[j, h] = keep.tile([P, HALF], F32, name=f"kept{j}{h}")
+                    nc.scalar.copy(kept[j, h][:], back[j, h][:])
 
         def finish(j):
             cols = slice(P * j, P * (j + 1))
@@ -177,36 +210,38 @@ def tile_attend_bvcrossed_s_kernel(tc, query, qs, grows, keys_words, keys_scales
             edges = (0, 512, 768, 1024) if j == 3 else (0, 512, 1024)
             for a, b in zip(edges, edges[1:]):
                 h = a // HALF
-                nc.vector.tensor_tensor(res[j][:, a:b], back[j, h][:, a - HALF * h : b - HALF * h], window[j][:, a:b], ALU.add)
+                if j < 3:
+                    nc.gpsimd.tensor_tensor(res[j][:, a:b], kept[j, h][:], window[j][:, a:b], ALU.add)
+                else:
+                    nc.vector.tensor_tensor(res[j][:, a:b], back[j, h][:, a - HALF * h : b - HALF * h], window[j][:, a:b], ALU.add)
                 nc.sync.dma_start(out=out[cols, a:b], in_=res[j][:, a:b])
 
         product(0)
         gather(1)
-        grows_block(1)
-        product(1)
+        for j in (1, 2, 3):
+            grows_block(j)
+            product(j)
+        faded_on_gpsimd(0)
         chain(0)
-        chain(1)
-        grows_block(2)
-        grows_block(3)
-        product(2)
-        product(3)
-        faded(0)
-        turn_back(0)
-        faded(1)
-        turn_back(1)
+        factor(1)
         scatter(0)
+        chain(1)
+        gather(2)
         scatter(1)
         finish(0)
-        gather(2)
-        faded(2)
-        turn_back(2)
-        chain(2)
+        faded(1)
+        turn_back(1)
+        factor(2)
         gather(3)
+        chain(2)
+        factor(3)
         scatter(2)
         finish(1)
+        faded(2)
+        turn_back(2)
+        chain(3)
+        scatter(3)
+        finish(2)
         faded(3)
         turn_back(3)
-        chain(3)
-        finish(2)
-        scatter(3)
         finish(3)

from contextlib import ExitStack

import concourse.mybir as mybir
from concourse.masks import make_identity

D, E, T, I, Q = 512, 512, 1024, 256, 512
FLOPS = 2 * D * Q * I + 2 * Q * E * I

F32 = mybir.dt.float32
BF16 = mybir.dt.bfloat16
I32 = mybir.dt.int32
U32 = mybir.dt.uint32
U16 = mybir.dt.uint16
U8 = mybir.dt.uint8
FP8X4 = mybir.dt.float8_e4m3fn_x4
FP4X4 = mybir.dt.float4_e2m1fn_x4
ACT = mybir.ActivationFunctionType
ALU = mybir.AluOpType
AXIS = mybir.AxisListType

P = 128
PACK = 4
HALF = 512


def tile_attend_bvcrossed_s_kernel(tc, query, qs, grows, keys_words, keys_scales, cross, share, sg, old, fade, offs, offs2, out):
    nc = tc.nc
    with ExitStack() as ctx:
        lists = ctx.enter_context(tc.tile_pool(name="lists", bufs=1))
        keep = ctx.enter_context(tc.tile_pool(name="keep", bufs=1))
        psum = ctx.enter_context(tc.psum_pool(name="psum", bufs=1))
        psum2 = ctx.enter_context(tc.psum_pool(name="psum2", bufs=2))

        key_scales = keep.tile([P, T], U8, name="key_scales", align_bytes=64)
        nc.gpsimd.memset(key_scales[:].bitcast(I32), 0)
        warm = keep.tile([P, 1], F32, name="warm")
        nc.gpsimd.memset(warm[:], 0.0)
        rows = keep.tile([P, P], F32, name="rows")
        nc.gpsimd.memset(rows[:], 0.0)
        key_words = keep.tile([P, T], U16, name="key_words", align_bytes=64)
        nc.sync.dma_start(out=key_words[:].bitcast(I32), in_=keys_words[0].bitcast(I32))
        offs_t = lists.tile([P, I // 16], U16, name="offs_t")
        nc.sync.dma_start(offs_t[:], offs)
        for quad in range(4):
            nc.sync.dma_start(out=key_scales[32 * quad : 32 * quad + 4, :].bitcast(I32), in_=keys_scales[0, 4 * quad : 4 * quad + 4, :].bitcast(I32))
        q_view = query.rearrange("(p j) q -> p j q", j=PACK)
        q_raw = []
        for h in range(2):
            t = keep.tile([P, PACK, Q // 2], F32, name=f"q_raw{h}")
            nc.sync.dma_start(out=t[:], in_=q_view[:, :, h * (Q // 2) : (h + 1) * (Q // 2)])
            q_raw.append(t)
        nc.sync.dma_start(out=rows[0:8, :], in_=fade.rearrange("o (b t) -> (o b) t", t=P))
        nc.sync.dma_start(out=rows[8:12, :], in_=share.rearrange("(j p) o -> j (p o)", p=P))
        nc.sync.dma_start(out=rows[12:14, :], in_=sg.rearrange("o (b t) -> (o b) t", t=P))
        nc.sync.dma_start(out=rows[16:20, :].rearrange("r (b c) -> r b c", c=8), in_=qs.rearrange("(b r c) o -> r b (c o)", r=PACK, c=8))
        offs2_t = lists.tile([P, I // 16], U16, name="offs2_t")
        nc.sync.dma_start(offs2_t[:], offs2)
        cross_t = [keep.tile([P, T], F32, name=f"cross{j}") for j in range(4)]
        old_t = [keep.tile([P, T], F32, name=f"old{j}") for j in range(4)]
        nc.sync.dma_start(out=cross_t[0][:], in_=cross[0:P, :])
        g_raw = keep.tile([P, PACK, E], F32, name="g_raw")
        g_view = grows.rearrange("(b r c) e -> r b c e", r=PACK, c=8)
        for r in range(PACK):
            nc.sync.dma_start(out=g_raw[:, r, :], in_=g_view[r])
        for j in range(1, 4):
            nc.sync.dma_start(out=cross_t[j][:], in_=cross[P * j : P * (j + 1), :])
        for j in range(4):
            nc.sync.dma_start(out=old_t[j][:], in_=old[P * j : P * (j + 1), :])

        nc.scalar.activation(warm[:], warm[:], ACT.Exp)
        ident = keep.tile([P, P], F32, name="ident")
        make_identity(nc, ident[:])
        gf = []
        for j in range(3):
            g = keep.tile([P, T], F32, name=f"gf{j}")
            nc.gpsimd.memset(g[:], 0.0)
            gf.append(g)

        kg = keep.tile([P, I], U16, name="kg", align_bytes=64)
        nc.vector.tensor_copy(kg[:], key_words[:].indirect(offs_t[:]))
        ksg = keep.tile([P, I], U8, name="ksg", align_bytes=64)
        nc.vector.tensor_copy(ksg[:], key_scales[:].indirect(offs_t[:]))

        q_bf = keep.tile([P, PACK, P, PACK], BF16, name="q_bf", align_bytes=64)
        def deal(copy, h, r):
            dst = q_bf[:, r, 64 * h : 64 * (h + 1), :].rearrange("p (b c i) j -> p b c j i", c=2, i=4)
            src = q_raw[h][:].rearrange("p j (b r c i) -> p r b c j i", r=PACK, c=2, i=4)[:, r]
            copy(dst, src)

        for r in range(PACK):
            deal(nc.scalar.copy, 0, r)
        deal(nc.scalar.copy, 1, 3)
        deal(nc.vector.tensor_copy, 1, 0)

        q_codes = keep.tile([P, Q], U32, name="q_codes", align_bytes=64)
        q_scales = keep.tile([P, Q], U8, name="q_scales", align_bytes=64)
        negmax = keep.tile([P, PACK], F32, name="negmax")
        sums = keep.tile([P, PACK], F32, name="sums")
        p_t = keep.tile([P, PACK, I], F32, name="p_t")
        scores = []
        for r in range(PACK):
            cols = slice(P * r, P * (r + 1))
            if r < 2:
                deal(nc.vector.tensor_copy, 1, r + 1)
            nc.vector.quantize_mx(out=q_codes[:, cols].bitcast(FP8X4), scales=q_scales[:, cols], in_=q_bf[:, r].rearrange("p s j -> p (s j)"))
            a = psum.tile([P, HALF], F32, name=f"bank{r}", tag=f"bank{r}")
            nc.tensor.matmul_mx(out=a[:, 0:I], lhsT=q_codes[:, cols].bitcast(FP8X4), lhsT_scale=q_scales[:, cols], rhs=kg[:].bitcast(FP4X4), rhs_scale=ksg[:], start=True, stop=True)
            scores.append(a)
        nc.tensor.transpose(scores[3][:, I : I + P], rows[:], ident[:])
        cols_t = keep.tile([P, 20], F32, name="cols_t")
        nc.scalar.copy(cols_t[:], scores[3][:, I : I + 20])
        spread = psum.tile([P, 2, I], F32, name="spread", tag="bank5")
        for c in range(2):
            nc.tensor.transpose(spread[:, 0, P * c : P * (c + 1)], cols_t[:, 12 + c : 13 + c].to_broadcast([P, P]), ident[:])

        for r in range(PACK):
            nc.vector.tensor_reduce(negmax[:, r : r + 1], scores[r][:, 0:I], AXIS.X, ALU.max, negate=True)
            nc.scalar.activation(p_t[:, r, :], scores[r][:, 0:I], ACT.Exp, bias=negmax[:, r : r + 1], scale=1.0, accum_out=sums[:, r : r + 1])

        g_bf = keep.tile([P, E, PACK], BF16, name="g_bf", align_bytes=64)
        g_codes = keep.tile([P, E], U32, name="g_codes", align_bytes=64)
        g_scales = keep.tile([P, E], U8, name="g_scales", align_bytes=64)

        def grows_block(j):
            cols = slice(P * j, P * (j + 1))
            nc.scalar.copy(g_bf[:, cols, :].rearrange("p (c i) r -> p c r i", i=4), g_raw[:, :, cols].rearrange("p r (c i) -> p c r i", i=4))
            nc.vector.quantize_mx(out=g_codes[:, cols].bitcast(FP8X4), scales=g_scales[:, cols], in_=g_bf[:, cols, :].rearrange("p e r -> p (e r)"))

        cg = {}

        def gather(j):
            cg[j] = keep.tile([P, I], F32, name=f"cg{j}")
            nc.vector.tensor_copy(cg[j][:], cross_t[j][:].indirect(offs2_t[:]))

        fac = {}

        def factor(j):
            fac[j] = keep.tile([P, I], F32, name=f"fac{j}")
            nc.vector.scalar_tensor_tensor(fac[j][:], cg[j][:], cols_t[:, 8 + j : 9 + j], spread[:, 0, :], ALU.add, ALU.mult)

        rinv = keep.tile([P, PACK], F32, name="rinv")
        w_rows = keep.tile([P, PACK, I], BF16, name="w_rows")
        for r0 in (0, 2):
            nc.vector.reciprocal(rinv[:, r0 : r0 + 2], sums[:, r0 : r0 + 2])
            if r0 == 0:
                gather(0)
            for r in (r0, r0 + 1):
                nc.vector.tensor_scalar(w_rows[:, r, :], p_t[:, r, :], rinv[:, r : r + 1], cols_t[:, 16 + r : 17 + r], ALU.mult, ALU.mult)
        factor(0)
        w_bf = keep.tile([P, I, PACK], BF16, name="w_bf", align_bytes=64)
        nc.vector.tensor_copy(w_bf[:].rearrange("p (c i) r -> p c r i", i=4), w_rows[:].rearrange("p r (c i) -> p c r i", i=4))
        grows_block(0)
        w_codes = keep.tile([P, I], U32, name="w_codes", align_bytes=64)
        w_scales = keep.tile([P, I], U8, name="w_scales", align_bytes=64)
        nc.vector.quantize_mx(out=w_codes[:].bitcast(FP8X4), scales=w_scales[:], in_=w_bf[:].rearrange("p i r -> p (i r)"))

        c0, dx, back, res, faded_t, kept = {}, {}, {}, {}, {}, {}
        window = (gf[0], gf[1], gf[2], gf[0])

        def product(j):
            cols = slice(P * j, P * (j + 1))
            if j == 1:
                pair = psum.tile([P, 2, I], F32, name="c0_pair", tag="bank1")
                c0[1], c0[2] = pair[:, 0, :], pair[:, 1, :]
            elif j == 0:
                c0[j] = psum.tile([P, I], F32, name="c0_first", tag="bank0")[:]
            elif j == 3:
                c0[j] = spread[:, 1, :]
            nc.tensor.matmul_mx(out=c0[j], lhsT=g_codes[:, cols].bitcast(FP8X4), lhsT_scale=g_scales[:, cols], rhs=w_codes[:].bitcast(FP8X4), rhs_scale=w_scales[:], start=True, stop=True)

        def chain(j):
            dx[j] = keep.tile([P, I], F32, name=f"dx{j}")
            nc.vector.tensor_tensor(dx[j][:], c0[j], fac[j][:], ALU.mult)

        def scatter(j):
            nc.vector.tensor_copy(window[j][:].indirect(offs_t[:]), dx[j][:])

        def faded(j):
            for h in range(2):
                fwd = psum2.tile([P, HALF], F32, name="fwd", tag="fwd")
                for b in range(4):
                    nc.tensor.transpose(fwd[:, P * b : P * (b + 1)], old_t[j][:, HALF * h + P * b : HALF * h + P * (b + 1)], ident[:])
                faded_t[j, h] = keep.tile([P, HALF], F32, name=f"faded_t{j}{h}")
                for b in range(4):
                    nc.scalar.activation(faded_t[j, h][:, P * b : P * (b + 1)], fwd[:, P * b : P * (b + 1)], ACT.Copy, scale=cols_t[:, 4 * h + b : 4 * h + b + 1])

        def faded_on_gpsimd(j):
            fade_row = keep.tile([P, T], F32, name="fade_row")
            for h in range(2):
                fwd = psum2.tile([P, HALF], F32, name="fwd", tag="fwd")
                for b in range(4):
                    nc.tensor.transpose(fwd[:, P * b : P * (b + 1)], cols_t[:, 4 * h + b : 4 * h + b + 1].to_broadcast([P, P]), ident[:])
                half = slice(HALF * h, HALF * (h + 1))
                nc.scalar.copy(fade_row[:, half], fwd[:])
                kept[j, h] = keep.tile([P, HALF], F32, name=f"kept{j}{h}")
                nc.gpsimd.tensor_tensor(kept[j, h][:], old_t[j][:, half], fade_row[:, half], ALU.mult)

        def turn_back(j):
            for h in range(2):
                back[j, h] = psum.tile([P, HALF], F32, name=f"back{j}{h}", tag=f"bank{2 + (2 * j + h) % 3}")
                for b in range(4):
                    nc.tensor.transpose(back[j, h][:, P * b : P * (b + 1)], faded_t[j, h][:, P * b : P * (b + 1)], ident[:])
                if j < 3:
                    kept[j, h] = keep.tile([P, HALF], F32, name=f"kept{j}{h}")
                    nc.scalar.copy(kept[j, h][:], back[j, h][:])

        def finish(j):
            cols = slice(P * j, P * (j + 1))
            res[j] = keep.tile([P, T], F32, name=f"res{j}")
            edges = (0, 512, 768, 1024) if j == 3 else (0, 512, 1024)
            for a, b in zip(edges, edges[1:]):
                h = a // HALF
                if j < 3:
                    nc.gpsimd.tensor_tensor(res[j][:, a:b], kept[j, h][:], window[j][:, a:b], ALU.add)
                else:
                    nc.vector.tensor_tensor(res[j][:, a:b], back[j, h][:, a - HALF * h : b - HALF * h], window[j][:, a:b], ALU.add)
                nc.sync.dma_start(out=out[cols, a:b], in_=res[j][:, a:b])

        product(0)
        gather(1)
        for j in (1, 2, 3):
            grows_block(j)
            product(j)
        faded_on_gpsimd(0)
        chain(0)
        factor(1)
        scatter(0)
        chain(1)
        gather(2)
        scatter(1)
        finish(0)
        faded(1)
        turn_back(1)
        factor(2)
        gather(3)
        chain(2)
        factor(3)
        scatter(2)
        finish(1)
        faded(2)
        turn_back(2)
        chain(3)
        scatter(3)
        finish(2)
        faded(3)
        turn_back(3)
        finish(3)
